import numpy as np, ml_dtypes
CORES = [242,247,114,119]
N = 4
F = 256
BETA, LR = 0.75, 0.5
def setup_inputs(rng):
    return {"gr": rng.standard_normal((N, 128, N * F), dtype=np.float32).astype(ml_dtypes.bfloat16), "m": rng.standard_normal((N, 128, F), dtype=np.float32).astype(ml_dtypes.bfloat16), "w": rng.standard_normal((N, 128, F), dtype=np.float32).astype(ml_dtypes.bfloat16)}
def setup_inputs_big(rng):
    d = setup_inputs(rng)
    for k in ("gr", "m", "w"): d[k] = (d[k].astype(np.float32) * 1048576.0).astype(d[k].dtype)
    return d
def setup_inputs_small(rng):
    d = setup_inputs(rng)
    for k in ("gr", "m", "w"): d[k] = (d[k].astype(np.float32) * (1 / 1048576.0)).astype(d[k].dtype)
    return d
def setup_inputs_apart(rng):
    d = setup_inputs(rng)
    f = (10.0 ** rng.permutation(np.linspace(-1.5, 1.5, N))).astype(np.float32).reshape(N, 1, 1)
    for k in ("gr", "m", "w"): d[k] = (d[k].astype(np.float32) * f).astype(d[k].dtype)
    return d
def reference(gr, m, w):
    GR, M, W = gr.astype(np.float64), m.astype(np.float64), w.astype(np.float64)
    s = GR.sum(axis=0)
    m2 = np.stack([BETA * M[r] + s[:, F * r:F * r + F] for r in range(N)])
    w2 = np.concatenate([W[r] - LR * m2[r] for r in range(N)], axis=1)
    return {"y": np.broadcast_to(w2.astype(ml_dtypes.bfloat16), (N, 128, N * F)), "mo": m2.astype(ml_dtypes.bfloat16)}

@@ -1,0 +1,165 @@
+from concourse.bass import DstId, RemoteDMATransfer
+from concourse.mybir import AluOpType
+
+N = 4
+F = 256
+BETA, LR = 0.75, 0.5
+
+SCRATCH = {
+    "G": ("sbuf", [128, N * F], "bfloat16"),
+    "R": ("sbuf", [128, (N - 1) * F], "bfloat16"),
+    "Y": ("sbuf", [128, N * F], "bfloat16"),
+    "M": ("sbuf", [128, F], "bfloat16"),
+    "W": ("sbuf", [128, F], "bfloat16"),
+    "BM": ("sbuf", [128, F], "bfloat16"),
+    "MO": ("sbuf", [128, F], "bfloat16"),
+    "CB": ("sbuf", [128, F], "bfloat16"),
+    "CI": ("sbuf", [128, F], "bfloat16"),
+    "Z": ("sbuf", [128, 129], "bfloat16"),
+    "ZD": ("dram", [128 * 129], "bfloat16"),
+    "D": ("sbuf", [128, 128], "bfloat16"),
+    "P": ("psum", [128, F], "float32"),
+}
+SEMAPHORES = ["ld_g", "ld_m", "ld_w", "fill", "cst", "laid", "diag", "bm", "rs0", "rs1", "rs2", "pe", "wdone", "modone",
+              "ag_near", "ag_far", "sent", "st_near", "st_far", "st_mo"]
+
+
+def _one_chip(topo, a, b):
+    return topo.host(a) == topo.host(b) and topo.chip(a) == topo.chip(b)
+
+
+def _engines(mask):
+    return [e for e in range(mask.bit_length()) if (mask >> e) & 1]
+
+
+def _plan(topo, cores, src):
+    far = [d for d in cores if d != src and not _one_chip(topo, src, d)]
+    near = [d for d in cores if d != src and _one_chip(topo, src, d)]
+    plan, used, per = {}, [], 4
+    if far:
+        common = topo.mask(src, far[0])
+        for d in far[1:]:
+            common &= topo.mask(src, d)
+        used = _engines(common)
+        per = 1
+        while per * 2 * len(far) <= len(used):
+            per *= 2
+        for i, d in enumerate(far):
+            plan[d] = used[i * per:(i + 1) * per]
+    for d in near:
+        free = [e for e in _engines(topo.mask(src, d)) if e not in used]
+        free = free[::2] + free[1::2]
+        plan[d] = free[:per]
+        used = used + plan[d]
+    return plan
+
+
+def _bits(engines):
+    return sum(1 << e for e in engines)
+
+
+def _runs(blocks):
+    out = []
+    for b in sorted(blocks):
+        if out and out[-1][1] == b:
+            out[-1][1] = b + 1
+        else:
+            out.append([b, b + 1])
+    return out
+
+
+def rank_program(g, core, T, topo):
+    rank = T.rank_of(core)
+    if rank is None:
+        return
+    S = T.sem
+    cores = list(T.cores)
+    peers = [d for d in cores if d != core]
+    near = [d for d in peers if _one_chip(topo, core, d)]
+    far = [d for d in peers if not _one_chip(topo, core, d)]
+    plan = _plan(topo, cores, core)
+    own = slice(rank * F, (rank + 1) * F)
+
+    def slot(sender_rank, receiver_rank):
+        return (sender_rank - receiver_rank) % N - 1
+
+    def lands(sender):
+        return len(_plan(topo, cores, sender)[core])
+
+    g.vector.memset(T.Z[:, 0:1], -LR).then_inc(S.fill, 1)
+    g.vector.memset(T.Z[:, 1:129], 0.0).then_inc(S.fill, 1)
+    g.vector.memset(T.CB[:, :], BETA).then_inc(S.cst, 1)
+    g.vector.memset(T.CI[:, :], -1.0 / LR).then_inc(S.cst, 1)
+
+    g.sync.dma_start(T.G[:, :], T.gr[:, :]).then_inc(S.ld_g, 16)
+    g.sync.dma_start(T.M[:, :], T.m[:, :]).then_inc(S.ld_m, 16)
+    g.sync.dma_start(T.W[:, :], T.w[:, :]).then_inc(S.ld_w, 16)
+    g.scalar.wait_ge(S.fill, 2)
+    g.scalar.dma_start(T.ZD[:], T.Z[:, :]).then_inc(S.laid, 16)
+    g.scalar.wait_ge(S.laid, 16)
+    g.scalar.dma_start(T.D[:, :], T.ZD[0:128 * 128]).then_inc(S.diag, 16)
+
+    g.wait_ge(S.ld_g, 16)
+    trs = []
+    for d in far + near:
+        rid, pid = topo.addr(d, core)
+        rd = T.rank_of(d)
+        k = slot(rank, rd)
+        trs.append(RemoteDMATransfer(dst_ids=[DstId(rid=rid, pnc=pid)], dma_engine_mask=_bits(plan[d]),
+                                     remote_sem=S["rs%d" % k], src=T.G[:, rd * F:(rd + 1) * F],
+                                     dst=T.R[:, k * F:(k + 1) * F]))
+    g.remote_dma_fused(trs, local_sem=S.sent)
+    sent = sum(len(plan[d]) for d in peers)
+
+    g.vector.wait_ge(S.cst, 2)
+    g.vector.wait_ge(S.ld_m, 16)
+    g.vector.tensor_tensor(T.BM[:, :], T.M[:, :], T.CB[:, :], AluOpType.mult).then_inc(S.bm, 1)
+
+    g.tensor.wait_ge(S.diag, 16)
+    g.tensor.wait_ge(S.ld_g, 16)
+    g.tensor.matmul(T.P[:, :], T.D[:, :], T.G[:, own], start=True, stop=False)
+    g.tensor.wait_ge(S.bm, 1)
+    g.tensor.matmul(T.P[:, :], T.D[:, :], T.BM[:, :], start=False, stop=False)
+    order = near + far
+    for i, s in enumerate(order):
+        k = slot(T.rank_of(s), rank)
+        g.tensor.wait_ge(S["rs%d" % k], lands(s))
+        mm = g.tensor.matmul(T.P[:, :], T.D[:, :], T.R[:, k * F:(k + 1) * F], start=False, stop=(i == len(order) - 1))
+    mm.then_inc(S.pe, 1)
+
+    g.vector.wait_ge(S.ld_w, 16)
+    g.vector.wait_ge(S.pe, 1)
+    g.vector.tensor_tensor(T.Y[:, own], T.P[:, :], T.W[:, :], AluOpType.add).then_inc(S.wdone, 1)
+    g.vector.tensor_tensor(T.MO[:, :], T.P[:, :], T.CI[:, :], AluOpType.mult).then_inc(S.modone, 1)
+
+    g.wait_ge(S.wdone, 1)
+    trs = []
+    for d in far + near:
+        rid, pid = topo.addr(d, core)
+        trs.append(RemoteDMATransfer(dst_ids=[DstId(rid=rid, pnc=pid)], dma_engine_mask=_bits(plan[d]),
+                                     remote_sem=(S.ag_near if d in near else S.ag_far), src=T.Y[:, own],
+                                     dst=T.Y[:, own]))
+    g.remote_dma_fused(trs, local_sem=S.sent)
+    sent += sum(len(plan[d]) for d in peers)
+
+    g.scalar.wait_ge(S.modone, 1)
+    g.scalar.dma_start(T.mo[:, :], T.MO[:, :]).then_inc(S.st_mo, 16)
+    g.scalar.wait_ge(S.wdone, 1)
+    if near:
+        g.scalar.wait_ge(S.ag_near, sum(lands(s) for s in near))
+    n_near = 0
+    for a, b in _runs([rank] + [T.rank_of(s) for s in near]):
+        g.scalar.dma_start(T.y[:, a * F:b * F], T.Y[:, a * F:b * F]).then_inc(S.st_near, 16)
+        n_near += 16
+    n_far = 0
+    if far:
+        g.sync.wait_ge(S.ag_far, sum(lands(s) for s in far))
+        for a, b in _runs([T.rank_of(s) for s in far]):
+            g.sync.dma_start(T.y[:, a * F:b * F], T.Y[:, a * F:b * F]).then_inc(S.st_far, 16)
+            n_far += 16
+
+    g.wait_ge(S.sent, sent)
+    g.wait_ge(S.st_mo, 16)
+    g.wait_ge(S.st_near, n_near)
+    if far:
+        g.wait_ge(S.st_far, n_far)

@@ -7,55 +7,45 @@ BETA, LR = 0.75, 0.5
 
 SCRATCH = {
     "G": ("sbuf", [128, N * F], "bfloat16"),
+    "GS": ("sbuf", [128, 2 * F], "bfloat16"),
     "R": ("sbuf", [128, (N - 1) * F], "bfloat16"),
     "Y": ("sbuf", [128, N * F], "bfloat16"),
     "M": ("sbuf", [128, F], "bfloat16"),
     "W": ("sbuf", [128, F], "bfloat16"),
     "BM": ("sbuf", [128, F], "bfloat16"),
+    "W2": ("sbuf", [128, F], "bfloat16"),
     "MO": ("sbuf", [128, F], "bfloat16"),
-    "CB": ("sbuf", [128, F], "bfloat16"),
-    "CI": ("sbuf", [128, F], "bfloat16"),
-    "Z": ("sbuf", [128, 129], "bfloat16"),
-    "ZD": ("dram", [128 * 129], "bfloat16"),
     "D": ("sbuf", [128, 128], "bfloat16"),
-    "P": ("psum", [128, F], "float32"),
+    "P": ("psum", [128, 512], "float32"),
+    "Q": ("psum", [128, 512], "float32"),
 }
-SEMAPHORES = ["ld_g", "ld_m", "ld_w", "fill", "cst", "laid", "diag", "bm", "rs0", "rs1", "rs2", "pe", "wdone", "modone",
-              "ag_near", "ag_far", "sent", "st_near", "st_far", "st_mo"]
+SEMAPHORES = ["ld_f0", "ld_f1", "ld_own", "ld_m", "ld_w", "fill", "diag", "sc_f", "sc_n", "bm", "w2",
+              "rs_f0", "rs_f1", "rs_near", "pe_p", "pe_q", "x1", "x2", "x3", "wdone", "modone",
+              "ag_f0", "ag_f1", "ag_near", "sent_s", "sent_g0", "sent_g1", "st_f0", "st_f1", "st_own", "st_mo"]
 
 
 def _one_chip(topo, a, b):
     return topo.host(a) == topo.host(b) and topo.chip(a) == topo.chip(b)
 
 
-def _engines(mask):
-    return [e for e in range(mask.bit_length()) if (mask >> e) & 1]
+def _count(mask):
+    return sum((mask >> e) & 1 for e in range(mask.bit_length()))
 
 
-def _plan(topo, cores, src):
-    far = [d for d in cores if d != src and not _one_chip(topo, src, d)]
+def _far_order(topo, cores, src):
+    far = [d for d in cores if not _one_chip(topo, src, d)]
+    pos = [c for c in cores if _one_chip(topo, src, c)].index(src)
+    k = pos % len(far)
+    return far[k:] + far[:k]
+
+
+def _masks(topo, cores, src):
+    far = [d for d in cores if not _one_chip(topo, src, d)]
     near = [d for d in cores if d != src and _one_chip(topo, src, d)]
-    plan, used, per = {}, [], 4
-    if far:
-        common = topo.mask(src, far[0])
-        for d in far[1:]:
-            common &= topo.mask(src, d)
-        used = _engines(common)
-        per = 1
-        while per * 2 * len(far) <= len(used):
-            per *= 2
-        for i, d in enumerate(far):
-            plan[d] = used[i * per:(i + 1) * per]
-    for d in near:
-        free = [e for e in _engines(topo.mask(src, d)) if e not in used]
-        free = free[::2] + free[1::2]
-        plan[d] = free[:per]
-        used = used + plan[d]
-    return plan
-
-
-def _bits(engines):
-    return sum(1 << e for e in engines)
+    fm = topo.mask(src, far[0])
+    for d in far[1:]:
+        fm &= topo.mask(src, d)
+    return fm, topo.mask(src, near[0]) & ~fm
 
 
 def _runs(blocks):
@@ -74,92 +64,100 @@ def rank_program(g, core, T, topo):
         return
     S = T.sem
     cores = list(T.cores)
-    peers = [d for d in cores if d != core]
-    near = [d for d in peers if _one_chip(topo, core, d)]
-    far = [d for d in peers if not _one_chip(topo, core, d)]
-    plan = _plan(topo, cores, core)
-    own = slice(rank * F, (rank + 1) * F)
+    near = [d for d in cores if d != core and _one_chip(topo, core, d)][0]
+    first, second = _far_order(topo, cores, core)
+    fmask, nmask = _masks(topo, cores, core)
+    nf, nn = _count(fmask), _count(nmask)
+    comes = [[s for s in (first, second) if _far_order(topo, cores, s)[k] == core][0] for k in range(2)]
 
-    def slot(sender_rank, receiver_rank):
-        return (sender_rank - receiver_rank) % N - 1
+    def tr(d, mask, sem, src, dst):
+        rid, pid = topo.addr(d, core)
+        return RemoteDMATransfer(dst_ids=[DstId(rid=rid, pnc=pid)], dma_engine_mask=mask, remote_sem=sem, src=src, dst=dst)
 
-    def lands(sender):
-        return len(_plan(topo, cores, sender)[core])
+    def blk(t, b):
+        return t[:, b * F:(b + 1) * F]
 
-    g.vector.memset(T.Z[:, 0:1], -LR).then_inc(S.fill, 1)
-    g.vector.memset(T.Z[:, 1:129], 0.0).then_inc(S.fill, 1)
-    g.vector.memset(T.CB[:, :], BETA).then_inc(S.cst, 1)
-    g.vector.memset(T.CI[:, :], -1.0 / LR).then_inc(S.cst, 1)
+    P, Q = T.P[:, 0:F], T.Q[:, 0:F]
+    r_early, r_late, r_near = blk(T.R, 0), blk(T.R, 1), blk(T.R, 2)
 
-    g.sync.dma_start(T.G[:, :], T.gr[:, :]).then_inc(S.ld_g, 16)
+    g.sync.dma_start(blk(T.G, T.rank_of(first)), blk(T.gr, T.rank_of(first))).then_inc(S.ld_f0, 16)
+    g.sync.dma_start(blk(T.G, T.rank_of(second)), blk(T.gr, T.rank_of(second))).then_inc(S.ld_f1, 16)
+    n_own = 0
+    for a, b in _runs([rank, T.rank_of(near)]):
+        g.sync.dma_start(T.G[:, a * F:b * F], T.gr[:, a * F:b * F]).then_inc(S.ld_own, 16)
+        n_own += 16
     g.sync.dma_start(T.M[:, :], T.m[:, :]).then_inc(S.ld_m, 16)
     g.sync.dma_start(T.W[:, :], T.w[:, :]).then_inc(S.ld_w, 16)
-    g.scalar.wait_ge(S.fill, 2)
-    g.scalar.dma_start(T.ZD[:], T.Z[:, :]).then_inc(S.laid, 16)
-    g.scalar.wait_ge(S.laid, 16)
-    g.scalar.dma_start(T.D[:, :], T.ZD[0:128 * 128]).then_inc(S.diag, 16)
 
-    g.wait_ge(S.ld_g, 16)
-    trs = []
-    for d in far + near:
-        rid, pid = topo.addr(d, core)
-        rd = T.rank_of(d)
-        k = slot(rank, rd)
-        trs.append(RemoteDMATransfer(dst_ids=[DstId(rid=rid, pnc=pid)], dma_engine_mask=_bits(plan[d]),
-                                     remote_sem=S["rs%d" % k], src=T.G[:, rd * F:(rd + 1) * F],
-                                     dst=T.R[:, k * F:(k + 1) * F]))
-    g.remote_dma_fused(trs, local_sem=S.sent)
-    sent = sum(len(plan[d]) for d in peers)
+    g.vector.memset(T.D[:, :], -LR).then_inc(S.fill, 1)
+    g.wait_ge(S.fill, 1)
+    g.affine_select(T.D[:, :], T.D[:, :], [[-1, 128]], AluOpType.is_equal, 0.0, 0, 1).then_inc(S.diag, 1)
 
-    g.vector.wait_ge(S.cst, 2)
+    g.vector.wait_ge(S.ld_f1, 16)
+    g.vector.tensor_scalar(blk(T.GS, 0), blk(T.G, T.rank_of(second)), -LR, None, AluOpType.mult).then_inc(S.sc_f, 1)
+    g.vector.wait_ge(S.ld_own, n_own)
+    g.vector.tensor_scalar(blk(T.GS, 1), blk(T.G, T.rank_of(near)), -LR, None, AluOpType.mult).then_inc(S.sc_n, 1)
     g.vector.wait_ge(S.ld_m, 16)
-    g.vector.tensor_tensor(T.BM[:, :], T.M[:, :], T.CB[:, :], AluOpType.mult).then_inc(S.bm, 1)
-
-    g.tensor.wait_ge(S.diag, 16)
-    g.tensor.wait_ge(S.ld_g, 16)
-    g.tensor.matmul(T.P[:, :], T.D[:, :], T.G[:, own], start=True, stop=False)
-    g.tensor.wait_ge(S.bm, 1)
-    g.tensor.matmul(T.P[:, :], T.D[:, :], T.BM[:, :], start=False, stop=False)
-    order = near + far
-    for i, s in enumerate(order):
-        k = slot(T.rank_of(s), rank)
-        g.tensor.wait_ge(S["rs%d" % k], lands(s))
-        mm = g.tensor.matmul(T.P[:, :], T.D[:, :], T.R[:, k * F:(k + 1) * F], start=False, stop=(i == len(order) - 1))
-    mm.then_inc(S.pe, 1)
-
+    g.vector.tensor_scalar(T.BM[:, :], T.M[:, :], BETA, None, AluOpType.mult).then_inc(S.bm, 1)
     g.vector.wait_ge(S.ld_w, 16)
-    g.vector.wait_ge(S.pe, 1)
-    g.vector.tensor_tensor(T.Y[:, own], T.P[:, :], T.W[:, :], AluOpType.add).then_inc(S.wdone, 1)
-    g.vector.tensor_tensor(T.MO[:, :], T.P[:, :], T.CI[:, :], AluOpType.mult).then_inc(S.modone, 1)
+    g.vector.tensor_scalar(T.W2[:, :], T.W[:, :], -1.0 / LR, None, AluOpType.mult).then_inc(S.w2, 1)
+
+    g.wait_ge(S.ld_f0, 16)
+    g.remote_dma_fused([tr(first, fmask, S.rs_f0, blk(T.G, T.rank_of(first)), r_early)], local_sem=S.sent_s)
+    g.wait_ge(S.sc_f, 1)
+    g.remote_dma_fused([tr(second, fmask, S.rs_f1, blk(T.GS, 0), r_late)], local_sem=S.sent_s)
+    g.wait_ge(S.sc_n, 1)
+    g.remote_dma_fused([tr(near, nmask, S.rs_near, blk(T.GS, 1), r_near)], local_sem=S.sent_s)
+    sent_s = 2 * nf + nn
+
+    g.tensor.wait_ge(S.diag, 1)
+    g.tensor.wait_ge(S.ld_own, n_own)
+    g.tensor.matmul(P, T.D[:, :], blk(T.G, rank), start=True, stop=False)
+    g.tensor.matmul(Q, T.D[:, :], blk(T.G, rank), start=True, stop=False)
+    g.tensor.wait_ge(S.bm, 1)
+    g.tensor.matmul(P, T.D[:, :], T.BM[:, :], start=False, stop=False)
+    g.tensor.matmul(Q, T.D[:, :], T.BM[:, :], start=False, stop=False)
+    g.tensor.wait_ge(S.w2, 1)
+    g.tensor.matmul(P, T.D[:, :], T.W2[:, :], start=False, stop=False)
+    g.tensor.wait_ge(S.rs_f0, nf)
+    g.tensor.matmul(P, T.D[:, :], r_early, start=False, stop=True).then_inc(S.pe_p, 1)
+    g.tensor.matmul(Q, T.D[:, :], r_early, start=False, stop=True).then_inc(S.pe_q, 1)
+
+    g.vector.wait_ge(S.pe_p, 1)
+    g.vector.wait_ge(S.rs_near, nn)
+    g.vector.tensor_tensor(P, P, r_near, AluOpType.add).then_inc(S.x1, 1)
+    g.vector.wait_ge(S.x1, 1)
+    g.vector.wait_ge(S.rs_f1, nf)
+    g.vector.tensor_tensor(blk(T.Y, rank), P, r_late, AluOpType.add).then_inc(S.wdone, 1)
+    g.vector.wait_ge(S.pe_q, 1)
+    g.vector.tensor_tensor(Q, Q, r_near, AluOpType.add).then_inc(S.x2, 1)
+    g.vector.wait_ge(S.x2, 1)
+    g.vector.tensor_tensor(Q, Q, r_late, AluOpType.add).then_inc(S.x3, 1)
+    g.vector.wait_ge(S.x3, 1)
+    g.vector.tensor_scalar(T.MO[:, :], Q, -1.0 / LR, None, AluOpType.mult).then_inc(S.modone, 1)
 
     g.wait_ge(S.wdone, 1)
-    trs = []
-    for d in far + near:
-        rid, pid = topo.addr(d, core)
-        trs.append(RemoteDMATransfer(dst_ids=[DstId(rid=rid, pnc=pid)], dma_engine_mask=_bits(plan[d]),
-                                     remote_sem=(S.ag_near if d in near else S.ag_far), src=T.Y[:, own],
-                                     dst=T.Y[:, own]))
-    g.remote_dma_fused(trs, local_sem=S.sent)
-    sent += sum(len(plan[d]) for d in peers)
+    mine = blk(T.Y, rank)
+    g.remote_dma_fused([tr(first, fmask, S.ag_f0, mine, mine), tr(near, nmask, S.ag_near, mine, mine)],
+                       local_sem=S.sent_g0)
+    g.remote_dma_fused([tr(second, fmask, S.ag_f1, mine, mine)], local_sem=S.sent_g1)
 
+    for k, s in enumerate(comes):
+        g.sync.wait_ge(S["ag_f%d" % k], nf)
+        g.sync.dma_start(blk(T.y, T.rank_of(s)), blk(T.Y, T.rank_of(s))).then_inc(S["st_f%d" % k], 16)
+    g.scalar.wait_ge(S.sent_g0, nf + nn)
+    g.scalar.wait_ge(S.wdone, 1)
+    g.scalar.wait_ge(S.ag_near, nn)
+    n_st = 0
+    for a, b in _runs([rank, T.rank_of(near)]):
+        g.scalar.dma_start(T.y[:, a * F:b * F], T.Y[:, a * F:b * F]).then_inc(S.st_own, 16)
+        n_st += 16
     g.scalar.wait_ge(S.modone, 1)
     g.scalar.dma_start(T.mo[:, :], T.MO[:, :]).then_inc(S.st_mo, 16)
-    g.scalar.wait_ge(S.wdone, 1)
-    if near:
-        g.scalar.wait_ge(S.ag_near, sum(lands(s) for s in near))
-    n_near = 0
-    for a, b in _runs([rank] + [T.rank_of(s) for s in near]):
-        g.scalar.dma_start(T.y[:, a * F:b * F], T.Y[:, a * F:b * F]).then_inc(S.st_near, 16)
-        n_near += 16
-    n_far = 0
-    if far:
-        g.sync.wait_ge(S.ag_far, sum(lands(s) for s in far))
-        for a, b in _runs([T.rank_of(s) for s in far]):
-            g.sync.dma_start(T.y[:, a * F:b * F], T.Y[:, a * F:b * F]).then_inc(S.st_far, 16)
-            n_far += 16
 
-    g.wait_ge(S.sent, sent)
+    g.wait_ge(S.sent_s, sent_s)
+    g.wait_ge(S.sent_g1, nf)
+    g.wait_ge(S.st_own, n_st)
     g.wait_ge(S.st_mo, 16)
-    g.wait_ge(S.st_near, n_near)
-    if far:
-        g.wait_ge(S.st_far, n_far)
+    g.wait_ge(S.st_f0, 16)
+    g.wait_ge(S.st_f1, 16)

@@ -7,8 +7,9 @@ BETA, LR = 0.75, 0.5
 
 SCRATCH = {
     "G": ("sbuf", [128, N * F], "bfloat16"),
-    "GS": ("sbuf", [128, 2 * F], "bfloat16"),
-    "R": ("sbuf", [128, (N - 1) * F], "bfloat16"),
+    "GS": ("sbuf", [128, F], "bfloat16"),
+    "U": ("sbuf", [128, F], "bfloat16"),
+    "R": ("sbuf", [128, 6 * F], "bfloat16"),
     "Y": ("sbuf", [128, N * F], "bfloat16"),
     "M": ("sbuf", [128, F], "bfloat16"),
     "W": ("sbuf", [128, F], "bfloat16"),
@@ -16,20 +17,22 @@ SCRATCH = {
     "W2": ("sbuf", [128, F], "bfloat16"),
     "MO": ("sbuf", [128, F], "bfloat16"),
     "D": ("sbuf", [128, 128], "bfloat16"),
+    "PU": ("psum", [128, 512], "float32"),
     "P": ("psum", [128, 512], "float32"),
     "Q": ("psum", [128, 512], "float32"),
+    "X": ("psum", [128, 512], "float32"),
 }
-SEMAPHORES = ["ld_f0", "ld_f1", "ld_own", "ld_m", "ld_w", "fill", "diag", "sc_f", "sc_n", "bm", "w2",
-              "rs_f0", "rs_f1", "rs_near", "pe_p", "pe_q", "x1", "x2", "x3", "wdone", "modone",
-              "ag_f0", "ag_f1", "ag_near", "sent_s", "sent_g0", "sent_g1", "st_f0", "st_f1", "st_own", "st_mo"]
+SEMAPHORES = ["ld_f0", "ld_f1", "ld_own", "ld_m", "ld_w", "fill", "diag", "sc_f", "bm", "w2",
+              "rs_f0", "rs_f1", "rs_near", "rs_e", "rs_u", "pe_u", "pe_p", "pe_q", "pe_x", "udone", "q1",
+              "wdone", "modone", "xdone", "ag_f", "ag_near", "sent_s", "sent_g", "st_f", "st_own", "st_mo", "st_x"]
 
 
 def _one_chip(topo, a, b):
     return topo.host(a) == topo.host(b) and topo.chip(a) == topo.chip(b)
 
 
-def _count(mask):
-    return sum((mask >> e) & 1 for e in range(mask.bit_length()))
+def _bits(mask):
+    return [e for e in range(mask.bit_length()) if (mask >> e) & 1]
 
 
 def _far_order(topo, cores, src):
@@ -39,13 +42,20 @@ def _far_order(topo, cores, src):
     return far[k:] + far[:k]
 
 
+def _near(topo, cores, c):
+    return [d for d in cores if d != c and _one_chip(topo, c, d)][0]
+
+
+def _comes(topo, cores, c, k):
+    return [s for s in cores if not _one_chip(topo, s, c) and _far_order(topo, cores, s)[k] == c][0]
+
+
 def _masks(topo, cores, src):
     far = [d for d in cores if not _one_chip(topo, src, d)]
-    near = [d for d in cores if d != src and _one_chip(topo, src, d)]
     fm = topo.mask(src, far[0])
     for d in far[1:]:
         fm &= topo.mask(src, d)
-    return fm, topo.mask(src, near[0]) & ~fm
+    return fm, topo.mask(src, _near(topo, cores, src)) & ~fm
 
 
 def _runs(blocks):
@@ -64,11 +74,16 @@ def rank_program(g, core, T, topo):
         return
     S = T.sem
     cores = list(T.cores)
-    near = [d for d in cores if d != core and _one_chip(topo, core, d)][0]
+    near = _near(topo, cores, core)
     first, second = _far_order(topo, cores, core)
+    x_me = _comes(topo, cores, core, 1)
+    x_near = _comes(topo, cores, near, 1)
+    near_partner = _far_order(topo, cores, near)[1]
+    giver = _comes(topo, cores, core, 0)
     fmask, nmask = _masks(topo, cores, core)
-    nf, nn = _count(fmask), _count(nmask)
-    comes = [[s for s in (first, second) if _far_order(topo, cores, s)[k] == core][0] for k in range(2)]
+    nf, nn = len(_bits(fmask)), len(_bits(nmask))
+    n_lo = sum(1 << e for e in _bits(nmask)[:nn // 2])
+    n_hi = nmask & ~n_lo
 
     def tr(d, mask, sem, src, dst):
         rid, pid = topo.addr(d, core)
@@ -77,11 +92,15 @@ def rank_program(g, core, T, topo):
     def blk(t, b):
         return t[:, b * F:(b + 1) * F]
 
-    P, Q = T.P[:, 0:F], T.Q[:, 0:F]
-    r_early, r_late, r_near = blk(T.R, 0), blk(T.R, 1), blk(T.R, 2)
+    def gblk(c):
+        return blk(T.G, T.rank_of(c))
 
-    g.sync.dma_start(blk(T.G, T.rank_of(first)), blk(T.gr, T.rank_of(first))).then_inc(S.ld_f0, 16)
-    g.sync.dma_start(blk(T.G, T.rank_of(second)), blk(T.gr, T.rank_of(second))).then_inc(S.ld_f1, 16)
+    PU, P, Q, X = T.PU[:, 0:F], T.P[:, 0:F], T.Q[:, 0:F], T.X[:, 0:F]
+    r_early, r_late, r_near, r_nx, r_e, r_u = [blk(T.R, i) for i in range(6)]
+    D = T.D[:, :]
+
+    g.sync.dma_start(gblk(first), blk(T.gr, T.rank_of(first))).then_inc(S.ld_f0, 16)
+    g.sync.dma_start(gblk(second), blk(T.gr, T.rank_of(second))).then_inc(S.ld_f1, 16)
     n_own = 0
     for a, b in _runs([rank, T.rank_of(near)]):
         g.sync.dma_start(T.G[:, a * F:b * F], T.gr[:, a * F:b * F]).then_inc(S.ld_own, 16)
@@ -89,63 +108,75 @@ def rank_program(g, core, T, topo):
     g.sync.dma_start(T.M[:, :], T.m[:, :]).then_inc(S.ld_m, 16)
     g.sync.dma_start(T.W[:, :], T.w[:, :]).then_inc(S.ld_w, 16)
 
-    g.vector.memset(T.D[:, :], -LR).then_inc(S.fill, 1)
+    g.vector.memset(D, -LR).then_inc(S.fill, 1)
     g.wait_ge(S.fill, 1)
-    g.affine_select(T.D[:, :], T.D[:, :], [[-1, 128]], AluOpType.is_equal, 0.0, 0, 1).then_inc(S.diag, 1)
+    g.affine_select(D, D, [[-1, 128]], AluOpType.is_equal, 0.0, 0, 1).then_inc(S.diag, 1)
 
     g.vector.wait_ge(S.ld_f1, 16)
-    g.vector.tensor_scalar(blk(T.GS, 0), blk(T.G, T.rank_of(second)), -LR, None, AluOpType.mult).then_inc(S.sc_f, 1)
-    g.vector.wait_ge(S.ld_own, n_own)
-    g.vector.tensor_scalar(blk(T.GS, 1), blk(T.G, T.rank_of(near)), -LR, None, AluOpType.mult).then_inc(S.sc_n, 1)
+    g.vector.tensor_scalar(T.GS[:, :], gblk(second), -LR, None, AluOpType.mult).then_inc(S.sc_f, 1)
     g.vector.wait_ge(S.ld_m, 16)
     g.vector.tensor_scalar(T.BM[:, :], T.M[:, :], BETA, None, AluOpType.mult).then_inc(S.bm, 1)
     g.vector.wait_ge(S.ld_w, 16)
     g.vector.tensor_scalar(T.W2[:, :], T.W[:, :], -1.0 / LR, None, AluOpType.mult).then_inc(S.w2, 1)
+    g.vector.wait_ge(S.pe_u, 1)
+    g.vector.tensor_copy(T.U[:, :], PU).then_inc(S.udone, 1)
 
     g.wait_ge(S.ld_f0, 16)
-    g.remote_dma_fused([tr(first, fmask, S.rs_f0, blk(T.G, T.rank_of(first)), r_early)], local_sem=S.sent_s)
+    g.remote_dma_fused([tr(first, fmask, S.rs_f0, gblk(first), r_early)], local_sem=S.sent_s)
     g.wait_ge(S.sc_f, 1)
-    g.remote_dma_fused([tr(second, fmask, S.rs_f1, blk(T.GS, 0), r_late)], local_sem=S.sent_s)
-    g.wait_ge(S.sc_n, 1)
-    g.remote_dma_fused([tr(near, nmask, S.rs_near, blk(T.GS, 1), r_near)], local_sem=S.sent_s)
-    sent_s = 2 * nf + nn
+    g.wait_ge(S.ld_f1, 16)
+    g.wait_ge(S.ld_own, n_own)
+    g.remote_dma_fused([tr(second, fmask, S.rs_f1, T.GS[:, :], r_late),
+                        tr(near, n_lo, S.rs_near, gblk(near), r_near),
+                        tr(near, n_hi, S.rs_near, gblk(x_near), r_nx)], local_sem=S.sent_s)
+    g.remote_dma_fused([tr(near_partner, fmask, S.rs_e, gblk(near), r_e)], local_sem=S.sent_s)
+    g.wait_ge(S.udone, 1)
+    g.remote_dma_fused([tr(second, fmask, S.rs_u, T.U[:, :], r_u)], local_sem=S.sent_s)
+    sent_s = 4 * nf + nn
 
     g.tensor.wait_ge(S.diag, 1)
+    g.tensor.wait_ge(S.ld_f0, 16)
+    g.tensor.wait_ge(S.ld_f1, 16)
     g.tensor.wait_ge(S.ld_own, n_own)
-    g.tensor.matmul(P, T.D[:, :], blk(T.G, rank), start=True, stop=False)
-    g.tensor.matmul(Q, T.D[:, :], blk(T.G, rank), start=True, stop=False)
+    g.tensor.matmul(PU, D, gblk(core), start=True, stop=False)
+    g.tensor.matmul(P, D, gblk(core), start=True, stop=False)
+    g.tensor.matmul(Q, D, gblk(core), start=True, stop=False)
+    g.tensor.matmul(X, D, gblk(x_me), start=True, stop=False)
     g.tensor.wait_ge(S.bm, 1)
-    g.tensor.matmul(P, T.D[:, :], T.BM[:, :], start=False, stop=False)
-    g.tensor.matmul(Q, T.D[:, :], T.BM[:, :], start=False, stop=False)
+    g.tensor.matmul(PU, D, T.BM[:, :], start=False, stop=False)
+    g.tensor.matmul(P, D, T.BM[:, :], start=False, stop=False)
+    g.tensor.matmul(Q, D, T.BM[:, :], start=False, stop=False)
     g.tensor.wait_ge(S.w2, 1)
-    g.tensor.matmul(P, T.D[:, :], T.W2[:, :], start=False, stop=False)
+    g.tensor.matmul(PU, D, T.W2[:, :], start=False, stop=True).then_inc(S.pe_u, 1)
+    g.tensor.matmul(P, D, T.W2[:, :], start=False, stop=False)
+    g.tensor.wait_ge(S.rs_near, nn)
+    g.tensor.matmul(P, D, r_near, start=False, stop=False)
     g.tensor.wait_ge(S.rs_f0, nf)
-    g.tensor.matmul(P, T.D[:, :], r_early, start=False, stop=True).then_inc(S.pe_p, 1)
-    g.tensor.matmul(Q, T.D[:, :], r_early, start=False, stop=True).then_inc(S.pe_q, 1)
+    g.tensor.matmul(P, D, r_early, start=False, stop=True).then_inc(S.pe_p, 1)
+    g.tensor.matmul(Q, D, r_near, start=False, stop=False)
+    g.tensor.matmul(Q, D, r_early, start=False, stop=True).then_inc(S.pe_q, 1)
+    g.tensor.matmul(X, D, r_nx, start=False, stop=False)
+    g.tensor.wait_ge(S.rs_e, nf)
+    g.tensor.matmul(X, D, r_e, start=False, stop=True).then_inc(S.pe_x, 1)
 
     g.vector.wait_ge(S.pe_p, 1)
-    g.vector.wait_ge(S.rs_near, nn)
-    g.vector.tensor_tensor(P, P, r_near, AluOpType.add).then_inc(S.x1, 1)
-    g.vector.wait_ge(S.x1, 1)
     g.vector.wait_ge(S.rs_f1, nf)
     g.vector.tensor_tensor(blk(T.Y, rank), P, r_late, AluOpType.add).then_inc(S.wdone, 1)
     g.vector.wait_ge(S.pe_q, 1)
-    g.vector.tensor_tensor(Q, Q, r_near, AluOpType.add).then_inc(S.x2, 1)
-    g.vector.wait_ge(S.x2, 1)
-    g.vector.tensor_tensor(Q, Q, r_late, AluOpType.add).then_inc(S.x3, 1)
-    g.vector.wait_ge(S.x3, 1)
+    g.vector.tensor_tensor(Q, Q, r_late, AluOpType.add).then_inc(S.q1, 1)
+    g.vector.wait_ge(S.q1, 1)
     g.vector.tensor_scalar(T.MO[:, :], Q, -1.0 / LR, None, AluOpType.mult).then_inc(S.modone, 1)
+    g.vector.wait_ge(S.pe_x, 1)
+    g.vector.wait_ge(S.rs_u, nf)
+    g.vector.tensor_tensor(blk(T.Y, T.rank_of(x_me)), X, r_u, AluOpType.add).then_inc(S.xdone, 1)
 
     g.wait_ge(S.wdone, 1)
     mine = blk(T.Y, rank)
-    g.remote_dma_fused([tr(first, fmask, S.ag_f0, mine, mine), tr(near, nmask, S.ag_near, mine, mine)],
-                       local_sem=S.sent_g0)
-    g.remote_dma_fused([tr(second, fmask, S.ag_f1, mine, mine)], local_sem=S.sent_g1)
+    g.remote_dma_fused([tr(first, fmask, S.ag_f, mine, mine), tr(near, nmask, S.ag_near, mine, mine)],
+                       local_sem=S.sent_g)
 
-    for k, s in enumerate(comes):
-        g.sync.wait_ge(S["ag_f%d" % k], nf)
-        g.sync.dma_start(blk(T.y, T.rank_of(s)), blk(T.Y, T.rank_of(s))).then_inc(S["st_f%d" % k], 16)
-    g.scalar.wait_ge(S.sent_g0, nf + nn)
+    g.sync.wait_ge(S.ag_f, nf)
+    g.sync.dma_start(blk(T.y, T.rank_of(giver)), blk(T.Y, T.rank_of(giver))).then_inc(S.st_f, 16)
     g.scalar.wait_ge(S.wdone, 1)
     g.scalar.wait_ge(S.ag_near, nn)
     n_st = 0
@@ -154,10 +185,12 @@ def rank_program(g, core, T, topo):
         n_st += 16
     g.scalar.wait_ge(S.modone, 1)
     g.scalar.dma_start(T.mo[:, :], T.MO[:, :]).then_inc(S.st_mo, 16)
+    g.scalar.wait_ge(S.xdone, 1)
+    g.scalar.dma_start(blk(T.y, T.rank_of(x_me)), blk(T.Y, T.rank_of(x_me))).then_inc(S.st_x, 16)
 
     g.wait_ge(S.sent_s, sent_s)
-    g.wait_ge(S.sent_g1, nf)
+    g.wait_ge(S.sent_g, nf + nn)
     g.wait_ge(S.st_own, n_st)
     g.wait_ge(S.st_mo, 16)
-    g.wait_ge(S.st_f0, 16)
-    g.wait_ge(S.st_f1, 16)
+    g.wait_ge(S.st_x, 16)
+    g.wait_ge(S.st_f, 16)

from concourse.bass import DstId, RemoteDMATransfer
from concourse.mybir import AluOpType

N = 4
F = 256
BETA, LR = 0.75, 0.5

SCRATCH = {
    "G": ("sbuf", [128, N * F], "bfloat16"),
    "GS": ("sbuf", [128, F], "bfloat16"),
    "U": ("sbuf", [128, F], "bfloat16"),
    "R": ("sbuf", [128, 6 * F], "bfloat16"),
    "Y": ("sbuf", [128, N * F], "bfloat16"),
    "M": ("sbuf", [128, F], "bfloat16"),
    "W": ("sbuf", [128, F], "bfloat16"),
    "BM": ("sbuf", [128, F], "bfloat16"),
    "W2": ("sbuf", [128, F], "bfloat16"),
    "MO": ("sbuf", [128, F], "bfloat16"),
    "D": ("sbuf", [128, 128], "bfloat16"),
    "PU": ("psum", [128, 512], "float32"),
    "P": ("psum", [128, 512], "float32"),
    "Q": ("psum", [128, 512], "float32"),
    "X": ("psum", [128, 512], "float32"),
}
SEMAPHORES = ["ld_f0", "ld_f1", "ld_own", "ld_m", "ld_w", "fill", "diag", "sc_f", "bm", "w2",
              "rs_f0", "rs_f1", "rs_near", "rs_e", "rs_u", "pe_u", "pe_p", "pe_q", "pe_x", "udone", "q1",
              "wdone", "modone", "xdone", "ag_f", "ag_near", "sent_s", "sent_g", "st_f", "st_own", "st_mo", "st_x"]


def _one_chip(topo, a, b):
    return topo.host(a) == topo.host(b) and topo.chip(a) == topo.chip(b)


def _bits(mask):
    return [e for e in range(mask.bit_length()) if (mask >> e) & 1]


def _far_order(topo, cores, src):
    far = [d for d in cores if not _one_chip(topo, src, d)]
    pos = [c for c in cores if _one_chip(topo, src, c)].index(src)
    k = pos % len(far)
    return far[k:] + far[:k]


def _near(topo, cores, c):
    return [d for d in cores if d != c and _one_chip(topo, c, d)][0]


def _comes(topo, cores, c, k):
    return [s for s in cores if not _one_chip(topo, s, c) and _far_order(topo, cores, s)[k] == c][0]


def _masks(topo, cores, src):
    far = [d for d in cores if not _one_chip(topo, src, d)]
    fm = topo.mask(src, far[0])
    for d in far[1:]:
        fm &= topo.mask(src, d)
    return fm, topo.mask(src, _near(topo, cores, src)) & ~fm


def _runs(blocks):
    out = []
    for b in sorted(blocks):
        if out and out[-1][1] == b:
            out[-1][1] = b + 1
        else:
            out.append([b, b + 1])
    return out


def rank_program(g, core, T, topo):
    rank = T.rank_of(core)
    if rank is None:
        return
    S = T.sem
    cores = list(T.cores)
    near = _near(topo, cores, core)
    first, second = _far_order(topo, cores, core)
    x_me = _comes(topo, cores, core, 1)
    x_near = _comes(topo, cores, near, 1)
    near_partner = _far_order(topo, cores, near)[1]
    giver = _comes(topo, cores, core, 0)
    fmask, nmask = _masks(topo, cores, core)
    nf, nn = len(_bits(fmask)), len(_bits(nmask))
    n_lo = sum(1 << e for e in _bits(nmask)[:nn // 2])
    n_hi = nmask & ~n_lo

    def tr(d, mask, sem, src, dst):
        rid, pid = topo.addr(d, core)
        return RemoteDMATransfer(dst_ids=[DstId(rid=rid, pnc=pid)], dma_engine_mask=mask, remote_sem=sem, src=src, dst=dst)

    def blk(t, b):
        return t[:, b * F:(b + 1) * F]

    def gblk(c):
        return blk(T.G, T.rank_of(c))

    PU, P, Q, X = T.PU[:, 0:F], T.P[:, 0:F], T.Q[:, 0:F], T.X[:, 0:F]
    r_early, r_late, r_near, r_nx, r_e, r_u = [blk(T.R, i) for i in range(6)]
    D = T.D[:, :]

    g.sync.dma_start(gblk(first), blk(T.gr, T.rank_of(first))).then_inc(S.ld_f0, 16)
    g.sync.dma_start(gblk(second), blk(T.gr, T.rank_of(second))).then_inc(S.ld_f1, 16)
    n_own = 0
    for a, b in _runs([rank, T.rank_of(near)]):
        g.sync.dma_start(T.G[:, a * F:b * F], T.gr[:, a * F:b * F]).then_inc(S.ld_own, 16)
        n_own += 16
    g.sync.dma_start(T.M[:, :], T.m[:, :]).then_inc(S.ld_m, 16)
    g.sync.dma_start(T.W[:, :], T.w[:, :]).then_inc(S.ld_w, 16)

    g.vector.memset(D, -LR).then_inc(S.fill, 1)
    g.wait_ge(S.fill, 1)
    g.affine_select(D, D, [[-1, 128]], AluOpType.is_equal, 0.0, 0, 1).then_inc(S.diag, 1)

    g.vector.wait_ge(S.ld_f1, 16)
    g.vector.tensor_scalar(T.GS[:, :], gblk(second), -LR, None, AluOpType.mult).then_inc(S.sc_f, 1)
    g.vector.wait_ge(S.ld_m, 16)
    g.vector.tensor_scalar(T.BM[:, :], T.M[:, :], BETA, None, AluOpType.mult).then_inc(S.bm, 1)
    g.vector.wait_ge(S.ld_w, 16)
    g.vector.tensor_scalar(T.W2[:, :], T.W[:, :], -1.0 / LR, None, AluOpType.mult).then_inc(S.w2, 1)
    g.vector.wait_ge(S.pe_u, 1)
    g.vector.tensor_copy(T.U[:, :], PU).then_inc(S.udone, 1)

    g.wait_ge(S.ld_f0, 16)
    g.remote_dma_fused([tr(first, fmask, S.rs_f0, gblk(first), r_early)], local_sem=S.sent_s)
    g.wait_ge(S.sc_f, 1)
    g.wait_ge(S.ld_f1, 16)
    g.wait_ge(S.ld_own, n_own)
    g.remote_dma_fused([tr(second, fmask, S.rs_f1, T.GS[:, :], r_late),
                        tr(near, n_lo, S.rs_near, gblk(near), r_near),
                        tr(near, n_hi, S.rs_near, gblk(x_near), r_nx)], local_sem=S.sent_s)
    g.remote_dma_fused([tr(near_partner, fmask, S.rs_e, gblk(near), r_e)], local_sem=S.sent_s)
    g.wait_ge(S.udone, 1)
    g.remote_dma_fused([tr(second, fmask, S.rs_u, T.U[:, :], r_u)], local_sem=S.sent_s)
    sent_s = 4 * nf + nn

    g.tensor.wait_ge(S.diag, 1)
    g.tensor.wait_ge(S.ld_f0, 16)
    g.tensor.wait_ge(S.ld_f1, 16)
    g.tensor.wait_ge(S.ld_own, n_own)
    g.tensor.matmul(PU, D, gblk(core), start=True, stop=False)
    g.tensor.matmul(P, D, gblk(core), start=True, stop=False)
    g.tensor.matmul(Q, D, gblk(core), start=True, stop=False)
    g.tensor.matmul(X, D, gblk(x_me), start=True, stop=False)
    g.tensor.wait_ge(S.bm, 1)
    g.tensor.matmul(PU, D, T.BM[:, :], start=False, stop=False)
    g.tensor.matmul(P, D, T.BM[:, :], start=False, stop=False)
    g.tensor.matmul(Q, D, T.BM[:, :], start=False, stop=False)
    g.tensor.wait_ge(S.w2, 1)
    g.tensor.matmul(PU, D, T.W2[:, :], start=False, stop=True).then_inc(S.pe_u, 1)
    g.tensor.matmul(P, D, T.W2[:, :], start=False, stop=False)
    g.tensor.wait_ge(S.rs_near, nn)
    g.tensor.matmul(P, D, r_near, start=False, stop=False)
    g.tensor.wait_ge(S.rs_f0, nf)
    g.tensor.matmul(P, D, r_early, start=False, stop=True).then_inc(S.pe_p, 1)
    g.tensor.matmul(Q, D, r_near, start=False, stop=False)
    g.tensor.matmul(Q, D, r_early, start=False, stop=True).then_inc(S.pe_q, 1)
    g.tensor.matmul(X, D, r_nx, start=False, stop=False)
    g.tensor.wait_ge(S.rs_e, nf)
    g.tensor.matmul(X, D, r_e, start=False, stop=True).then_inc(S.pe_x, 1)

    g.vector.wait_ge(S.pe_p, 1)
    g.vector.wait_ge(S.rs_f1, nf)
    g.vector.tensor_tensor(blk(T.Y, rank), P, r_late, AluOpType.add).then_inc(S.wdone, 1)
    g.vector.wait_ge(S.pe_q, 1)
    g.vector.tensor_tensor(Q, Q, r_late, AluOpType.add).then_inc(S.q1, 1)
    g.vector.wait_ge(S.q1, 1)
    g.vector.tensor_scalar(T.MO[:, :], Q, -1.0 / LR, None, AluOpType.mult).then_inc(S.modone, 1)
    g.vector.wait_ge(S.pe_x, 1)
    g.vector.wait_ge(S.rs_u, nf)
    g.vector.tensor_tensor(blk(T.Y, T.rank_of(x_me)), X, r_u, AluOpType.add).then_inc(S.xdone, 1)

    g.wait_ge(S.wdone, 1)
    mine = blk(T.Y, rank)
    g.remote_dma_fused([tr(first, fmask, S.ag_f, mine, mine), tr(near, nmask, S.ag_near, mine, mine)],
                       local_sem=S.sent_g)

    g.sync.wait_ge(S.ag_f, nf)
    g.sync.dma_start(blk(T.y, T.rank_of(giver)), blk(T.Y, T.rank_of(giver))).then_inc(S.st_f, 16)
    g.scalar.wait_ge(S.wdone, 1)
    g.scalar.wait_ge(S.ag_near, nn)
    n_st = 0
    for a, b in _runs([rank, T.rank_of(near)]):
        g.scalar.dma_start(T.y[:, a * F:b * F], T.Y[:, a * F:b * F]).then_inc(S.st_own, 16)
        n_st += 16
    g.scalar.wait_ge(S.modone, 1)
    g.scalar.dma_start(T.mo[:, :], T.MO[:, :]).then_inc(S.st_mo, 16)
    g.scalar.wait_ge(S.xdone, 1)
    g.scalar.dma_start(blk(T.y, T.rank_of(x_me)), blk(T.Y, T.rank_of(x_me))).then_inc(S.st_x, 16)

    g.wait_ge(S.sent_s, sent_s)
    g.wait_ge(S.sent_g, nf + nn)
    g.wait_ge(S.st_own, n_st)
    g.wait_ge(S.st_mo, 16)
    g.wait_ge(S.st_x, 16)
    g.wait_ge(S.st_f, 16)
